import numpy as np
import ml_dtypes


def mxq(x, axis, fmt="e4m3"):
    dtype, down = {"e4m3": (ml_dtypes.float8_e4m3fn, 7), "e5m2": (ml_dtypes.float8_e5m2, 14)}[fmt]
    v = np.moveaxis(np.asarray(x, np.float32).astype(ml_dtypes.bfloat16).astype(np.float64), axis, -1)
    blocks = v.reshape(v.shape[:-1] + (-1, 32))
    amax = np.abs(blocks).max(-1, keepdims=True)
    byte = np.maximum(np.where(amax > 0, np.frexp(amax)[1] - 1 + 127, 0) - down, 1)
    scale = np.exp2(byte - 127.0)
    codes = (blocks / scale).astype(np.float32).astype(dtype).astype(np.float64)
    return np.moveaxis((codes * scale).reshape(v.shape), -1, axis)


WIDE = False


def mx_kscale(k):
    if not WIDE:
        return np.ones(k)
    levels = np.array([10, -10, 5, -5, 0])
    if k % 512:
        return np.exp2(np.random.permutation(np.resize(levels, k // 32))).repeat(32)
    a = np.empty((k // 512, 16))
    for p in range(k // 512):
        a[p, :8] = np.random.permutation(np.resize(levels, 8))
        for g in range(8):
            far = levels[np.abs(levels - a[p, g]) >= 10]
            a[p, g + 8] = far[np.random.randint(len(far))]
    return np.exp2(a.ravel()).repeat(32)


def f64(x):
    return np.asarray(x).astype(np.float64)


def striped(idx):
    return np.tile(np.asarray(idx).reshape(-1, 16).T, (8, 1)).astype(np.uint16)


def unstriped(offs):
    return offs[:16].T.reshape(-1).astype(np.int64)


O, G, T, D, M = 8, 512, 512, 1024, 128


def setup_inputs():
    n = np.random.standard_normal
    s = mx_kscale(D)[:, None]
    grid = lambda x: np.round(x * 32) / 32
    return {
        "cb": (grid(n((O, D, T))) / s).astype(np.float32),
        "w": (n((D, M)) * s / np.sqrt(O * D)).astype(np.float32),
        "norm": np.tile(np.random.randint(32, 129, G) / 64.0, (128, 1)).astype(np.float32),
        "offs": striped(np.random.randint(0, T, O * G)),
    }


def reference(cb, w, norm, offs):
    code = unstriped(offs).reshape(O, G)
    e = sum(f64(cb)[o][:, code[o]] for o in range(O)) * f64(norm)[:1]
    y = mxq(f64(w), 0, "e4m3").T @ mxq(e, 0, "e4m3")
    return y

@@ -1,0 +1,153 @@
+from contextlib import ExitStack
+
+import concourse.mybir as mybir
+
+O, G, T, D, M = 8, 512, 512, 1024, 128
+P = 128
+PASS = 512
+N_PASS = D // PASS
+FLOPS = 2 * D * M * G
+
+F32 = mybir.dt.float32
+BF16 = mybir.dt.bfloat16
+U32 = mybir.dt.uint32
+U16 = mybir.dt.uint16
+U8 = mybir.dt.uint8
+FP8X4 = mybir.dt.float8_e4m3fn_x4
+ADD = mybir.AluOpType.add
+MULT = mybir.AluOpType.mult
+COPY = mybir.ActivationFunctionType.Copy
+
+WINDOW = 688
+TABLE_WORDS = T + WINDOW
+N_TABLES = 8
+ON_GPSIMD = (5, 4)
+HALF = G // 2
+
+
+def tile_attend_aq_kernel(tc, cb, w, norm, offs, out):
+    nc = tc.nc
+    with ExitStack() as ctx:
+        keep = ctx.enter_context(tc.tile_pool(name="keep", bufs=1))
+        stage = ctx.enter_context(tc.tile_pool(name="stage", bufs=6))
+        ring = ctx.enter_context(tc.tile_pool(name="ring", bufs=16))
+        psum = ctx.enter_context(tc.psum_pool(name="psum", bufs=1))
+
+        lists = keep.tile([P, O * G // 16], U16, name="lists")
+        nc.sync.dma_start(lists[:], offs)
+
+        tables = [keep.tile([P, 2 * TABLE_WORDS], BF16, name=f"table{i}") for i in range(N_TABLES)]
+        for t in tables:
+            nc.gpsimd.memset(t[:, 4 * T :], 0.0)
+
+        norm_sb = keep.tile([P, G], F32, name="norm_sb")
+        w_raw = keep.tile([P, N_PASS, 4, M], F32, name="w_raw")
+        w_bf = keep.tile([P, N_PASS * M * 4], BF16, name="w_bf", align_bytes=64)
+        w_codes = keep.tile([P, N_PASS * M], U32, name="w_codes", align_bytes=64)
+        w_scales = keep.tile([P, N_PASS * M], U8, name="w_scales", align_bytes=64)
+
+        acc_g = [keep.tile([P, 4 * G], F32, name=f"acc_g{i}") for i in range(N_PASS)]
+        acc_v = [keep.tile([P, 4 * G], F32, name=f"acc_v{i}") for i in range(N_PASS)]
+        e_bf = [keep.tile([P, 4 * G], BF16, name=f"e_bf{i}", align_bytes=64) for i in range(N_PASS)]
+        e_codes = [keep.tile([P, G], U32, name=f"e_codes{i}", align_bytes=64) for i in range(N_PASS)]
+        e_scales = [keep.tile([P, G], U8, name=f"e_scales{i}", align_bytes=64) for i in range(N_PASS)]
+        banks = [psum.tile([M, HALF], F32, name=f"bank{i}") for i in range(2)]
+        out_sb = [keep.tile([M, HALF], F32, name=f"out_sb{i}") for i in range(2)]
+        gathered = {}
+
+        def load_and_gather(i, o):
+            step = O * i + o
+            raw = stage.tile([P, 4, T], F32, name="raw")
+            src = cb[o, PASS * i : PASS * (i + 1), :].rearrange("(p j) c -> p j c", j=4)
+            table = tables[step % N_TABLES]
+            if step == 0:
+                for h in range(2):
+                    nc.sync.dma_start(raw[:, 2 * h : 2 * h + 2, :], src[:, 2 * h : 2 * h + 2, :])
+                for h in range(2):
+                    dst = table[:, 2 * T * h : 2 * T * (h + 1)].rearrange("p (c e) -> p c e", e=2)
+                    part = raw[:, 2 * h : 2 * h + 2, :].rearrange("p e c -> p c e")
+                    if h == 0:
+                        nc.vector.tensor_copy(dst, part)
+                    else:
+                        nc.scalar.activation(dst, part, COPY)
+            else:
+                nc.sync.dma_start(raw[:], src)
+                for h in range(2):
+                    dst = table[:, 2 * T * h : 2 * T * (h + 1)].rearrange("p (c e) -> p c e", e=2)
+                    part = raw[:, 2 * h : 2 * h + 2, :].rearrange("p e c -> p c e")
+                    nc.scalar.activation(dst, part, COPY)
+            g = ring.tile([P, 4 * G], BF16, name="g")
+            offsets = lists[:, (G // 16) * o : (G // 16) * (o + 1)]
+            for h in range(2):
+                window = table[:, 2 * T * h : 2 * (T * h + WINDOW)].bitcast(U32)
+                nc.vector.tensor_copy(g[:, 2 * G * h : 2 * G * (h + 1)].bitcast(U32), window.indirect(offsets))
+            gathered[i, o] = g
+
+        def add_on(engine, dst, a, b):
+            for h in range(2):
+                s = slice(2 * G * h, 2 * G * (h + 1))
+                engine.tensor_tensor(dst[:, s], a[:, s], b[:, s], ADD)
+
+        def gpsimd_step(i, o):
+            if o == 1:
+                add_on(nc.gpsimd, acc_g[i], gathered[i, 0], gathered[i, 1])
+            elif 1 < o <= ON_GPSIMD[i]:
+                add_on(nc.gpsimd, acc_g[i], acc_g[i], gathered[i, o])
+
+        def scale_quantise(i, c0, c1):
+            n = c1 - c0
+            src = acc_v[i][:].rearrange("p (h c e) -> p c h e", h=2, e=2)[:, c0:c1]
+            by = norm_sb[:, c0:c1].unsqueeze(2).unsqueeze(3).to_broadcast([P, n, 2, 2])
+            dst = e_bf[i][:, 4 * c0 : 4 * c1].rearrange("p (c h e) -> p c h e", h=2, e=2)
+            nc.vector.tensor_tensor(dst, src, by, MULT)
+            nc.vector.quantize_mx(e_codes[i][:, c0:c1].bitcast(FP8X4), e_scales[i][:, c0:c1], e_bf[i][:, 4 * c0 : 4 * c1])
+
+        def multiply(i, b):
+            c = slice(HALF * b, HALF * (b + 1))
+            m = slice(M * i, M * (i + 1))
+            nc.tensor.matmul_mx(
+                out=banks[b][:],
+                lhsT=w_codes[:, m].bitcast(FP8X4),
+                lhsT_scale=w_scales[:, m],
+                rhs=e_codes[i][:, c].bitcast(FP8X4),
+                rhs_scale=e_scales[i][:, c],
+                start=(i == 0),
+                stop=(i == N_PASS - 1),
+            )
+
+        for o in range(O):
+            load_and_gather(0, o)
+            gpsimd_step(0, o)
+            if o == 2:
+                nc.sync.dma_start(w_raw[:], w.rearrange("(i p j) m -> p i j m", i=N_PASS, j=4))
+                nc.sync.dma_start(norm_sb[:], norm)
+            if o == 5:
+                nc.scalar.activation(
+                    w_bf[:].rearrange("p (i m j) -> p i m j", i=N_PASS, j=4),
+                    w_raw[:].rearrange("p i j m -> p i m j"),
+                    COPY,
+                )
+                nc.vector.quantize_mx(w_codes[:].bitcast(FP8X4), w_scales[:], w_bf[:])
+
+        for o in range(O):
+            load_and_gather(1, o)
+            gpsimd_step(1, o)
+            if o == 3:
+                add_on(nc.vector, acc_v[0], gathered[0, 6], gathered[0, 7])
+            if o == 4:
+                add_on(nc.vector, acc_v[0], acc_v[0], acc_g[0])
+            if o == 5:
+                scale_quantise(0, 0, G)
+                multiply(0, 0)
+                multiply(0, 1)
+            if o == 6:
+                add_on(nc.vector, acc_v[1], gathered[1, 5], gathered[1, 6])
+        add_on(nc.vector, acc_v[1], acc_v[1], acc_g[1])
+        halves = lambda t, b: t[:].rearrange("p (h c) -> p h c", h=2)[:, :, G * b : G * (b + 1)]
+        for b in range(2):
+            nc.vector.tensor_tensor(halves(acc_v[1], b), halves(acc_v[1], b), halves(gathered[1, 7], b), ADD)
+        for b in range(2):
+            scale_quantise(1, HALF * b, HALF * (b + 1))
+            multiply(1, b)
+            nc.scalar.activation(out_sb[b][:], banks[b][:], COPY)
+            nc.sync.dma_start(out[:, HALF * b : HALF * (b + 1)], out_sb[b][:])

@@ -1,6 +1,7 @@
 from contextlib import ExitStack
 
 import concourse.mybir as mybir
+from concourse.masks import make_identity
 
 O, G, T, D, M = 8, 512, 512, 1024, 128
 P = 128
@@ -21,7 +22,7 @@ COPY = mybir.ActivationFunctionType.Copy
 WINDOW = 688
 TABLE_WORDS = T + WINDOW
 N_TABLES = 8
-ON_GPSIMD = (5, 4)
+ON_GPSIMD = (4, 4)
 HALF = G // 2
 
 
@@ -32,6 +33,7 @@ def tile_attend_aq_kernel(tc, cb, w, norm, offs, out):
         stage = ctx.enter_context(tc.tile_pool(name="stage", bufs=6))
         ring = ctx.enter_context(tc.tile_pool(name="ring", bufs=16))
         psum = ctx.enter_context(tc.psum_pool(name="psum", bufs=1))
+        flips = ctx.enter_context(tc.psum_pool(name="flips", bufs=2))
 
         lists = keep.tile([P, O * G // 16], U16, name="lists")
         nc.sync.dma_start(lists[:], offs)
@@ -40,7 +42,10 @@ def tile_attend_aq_kernel(tc, cb, w, norm, offs, out):
         for t in tables:
             nc.gpsimd.memset(t[:, 4 * T :], 0.0)
 
+        identity = keep.tile([P, P], F32, name="identity")
+        make_identity(nc, identity[:])
         norm_sb = keep.tile([P, G], F32, name="norm_sb")
+        norm_ps = psum.tile([P, G], F32, name="norm_ps")
         w_raw = keep.tile([P, N_PASS, 4, M], F32, name="w_raw")
         w_bf = keep.tile([P, N_PASS * M * 4], BF16, name="w_bf", align_bytes=64)
         w_codes = keep.tile([P, N_PASS * M], U32, name="w_codes", align_bytes=64)
@@ -53,7 +58,26 @@ def tile_attend_aq_kernel(tc, cb, w, norm, offs, out):
         e_scales = [keep.tile([P, G], U8, name=f"e_scales{i}", align_bytes=64) for i in range(N_PASS)]
         banks = [psum.tile([M, HALF], F32, name=f"bank{i}") for i in range(2)]
         out_sb = [keep.tile([M, HALF], F32, name=f"out_sb{i}") for i in range(2)]
+        total = (acc_g[0], acc_v[1])
         gathered = {}
+
+        def through_tensor(dst, src):
+            turned = flips.tile([P, G], F32, name="turned")
+            for b in range(G // P):
+                s = slice(P * b, P * (b + 1))
+                nc.tensor.transpose(turned[:, s], src[:, s], identity[:])
+            back = stage.tile([P, G], F32, name="back")
+            nc.scalar.copy(back[:], turned[:])
+            for b in range(G // P):
+                s = slice(P * b, P * (b + 1))
+                nc.tensor.transpose(dst[:, s], back[:, s], identity[:])
+
+        def add_from_psum(dst, a, b):
+            for h in range(2):
+                s = slice(2 * G * h, 2 * G * (h + 1))
+                words = flips.tile([P, G], F32, name="words")
+                through_tensor(words, b[:, s].bitcast(F32))
+                nc.vector.tensor_tensor(dst[:, s], words[:].bitcast(BF16), a[:, s], ADD)
 
         def load_and_gather(i, o):
             step = O * i + o
@@ -96,8 +120,8 @@ def tile_attend_aq_kernel(tc, cb, w, norm, offs, out):
 
         def scale_quantise(i, c0, c1):
             n = c1 - c0
-            src = acc_v[i][:].rearrange("p (h c e) -> p c h e", h=2, e=2)[:, c0:c1]
-            by = norm_sb[:, c0:c1].unsqueeze(2).unsqueeze(3).to_broadcast([P, n, 2, 2])
+            src = total[i][:].rearrange("p (h c e) -> p c h e", h=2, e=2)[:, c0:c1]
+            by = norm_ps[:, c0:c1].unsqueeze(2).unsqueeze(3).to_broadcast([P, n, 2, 2])
             dst = e_bf[i][:, 4 * c0 : 4 * c1].rearrange("p (c h e) -> p c h e", h=2, e=2)
             nc.vector.tensor_tensor(dst, src, by, MULT)
             nc.vector.quantize_mx(e_codes[i][:, c0:c1].bitcast(FP8X4), e_scales[i][:, c0:c1], e_bf[i][:, 4 * c0 : 4 * c1])
@@ -121,6 +145,7 @@ def tile_attend_aq_kernel(tc, cb, w, norm, offs, out):
             if o == 2:
                 nc.sync.dma_start(w_raw[:], w.rearrange("(i p j) m -> p i j m", i=N_PASS, j=4))
                 nc.sync.dma_start(norm_sb[:], norm)
+                through_tensor(norm_ps, norm_sb)
             if o == 5:
                 nc.scalar.activation(
                     w_bf[:].rearrange("p (i m j) -> p i m j", i=N_PASS, j=4),
@@ -132,16 +157,16 @@ def tile_attend_aq_kernel(tc, cb, w, norm, offs, out):
         for o in range(O):
             load_and_gather(1, o)
             gpsimd_step(1, o)
-            if o == 3:
-                add_on(nc.vector, acc_v[0], gathered[0, 6], gathered[0, 7])
-            if o == 4:
-                add_on(nc.vector, acc_v[0], acc_v[0], acc_g[0])
+            if o == 0:
+                add_from_psum(acc_v[0], gathered[0, 6], gathered[0, 5])
+                add_from_psum(acc_v[0], acc_v[0], gathered[0, 7])
+                add_on(nc.gpsimd, acc_g[0], acc_g[0], acc_v[0])
             if o == 5:
                 scale_quantise(0, 0, G)
                 multiply(0, 0)
                 multiply(0, 1)
             if o == 6:
-                add_on(nc.vector, acc_v[1], gathered[1, 5], gathered[1, 6])
+                add_from_psum(acc_v[1], gathered[1, 6], gathered[1, 5])
         add_on(nc.vector, acc_v[1], acc_v[1], acc_g[1])
         halves = lambda t, b: t[:].rearrange("p (h c) -> p h c", h=2)[:, :, G * b : G * (b + 1)]
         for b in range(2):

@@ -20,9 +20,8 @@ MULT = mybir.AluOpType.mult
 COPY = mybir.ActivationFunctionType.Copy
 
 WINDOW = 688
-TABLE_WORDS = T + WINDOW
 N_TABLES = 8
-ON_GPSIMD = (4, 4)
+ON_GPSIMD = (5, 2)
 HALF = G // 2
 
 
@@ -33,19 +32,22 @@ def tile_attend_aq_kernel(tc, cb, w, norm, offs, out):
         stage = ctx.enter_context(tc.tile_pool(name="stage", bufs=6))
         ring = ctx.enter_context(tc.tile_pool(name="ring", bufs=16))
         psum = ctx.enter_context(tc.psum_pool(name="psum", bufs=1))
+        words_pool = ctx.enter_context(tc.psum_pool(name="words_pool", bufs=4))
         flips = ctx.enter_context(tc.psum_pool(name="flips", bufs=2))
 
         lists = keep.tile([P, O * G // 16], U16, name="lists")
-        nc.sync.dma_start(lists[:], offs)
 
-        tables = [keep.tile([P, 2 * TABLE_WORDS], BF16, name=f"table{i}") for i in range(N_TABLES)]
+        tables = [keep.tile([P, 2, 2 * WINDOW], BF16, name=f"table{i}") for i in range(N_TABLES)]
         for t in tables:
-            nc.gpsimd.memset(t[:, 4 * T :], 0.0)
+            nc.gpsimd.memset(t[:, :, 2 * T :].bitcast(U32), 0)
 
         identity = keep.tile([P, P], F32, name="identity")
         make_identity(nc, identity[:])
+        identity_bf = keep.tile([P, P], BF16, name="identity_bf")
+        make_identity(nc, identity_bf[:])
+        norm_turned = keep.tile([P, G], F32, name="norm_turned")
+        middle = [keep.tile([P, G], BF16, name=f"middle{i}") for i in range(2)]
         norm_sb = keep.tile([P, G], F32, name="norm_sb")
-        norm_ps = psum.tile([P, G], F32, name="norm_ps")
         w_raw = keep.tile([P, N_PASS, 4, M], F32, name="w_raw")
         w_bf = keep.tile([P, N_PASS * M * 4], BF16, name="w_bf", align_bytes=64)
         w_codes = keep.tile([P, N_PASS * M], U32, name="w_codes", align_bytes=64)
@@ -58,70 +60,104 @@ def tile_attend_aq_kernel(tc, cb, w, norm, offs, out):
         e_scales = [keep.tile([P, G], U8, name=f"e_scales{i}", align_bytes=64) for i in range(N_PASS)]
         banks = [psum.tile([M, HALF], F32, name=f"bank{i}") for i in range(2)]
         out_sb = [keep.tile([M, HALF], F32, name=f"out_sb{i}") for i in range(2)]
-        total = (acc_g[0], acc_v[1])
+        total = (acc_g[0], acc_v[0])
         gathered = {}
 
-        def through_tensor(dst, src):
+        def turn(src, dst):
             turned = flips.tile([P, G], F32, name="turned")
             for b in range(G // P):
                 s = slice(P * b, P * (b + 1))
                 nc.tensor.transpose(turned[:, s], src[:, s], identity[:])
+            nc.scalar.copy(dst[:], turned[:])
+
+        def half(t, h):
+            return t[:, 2 * G * h : 2 * G * (h + 1)]
+
+        def to_psum(src, h):
             back = stage.tile([P, G], F32, name="back")
-            nc.scalar.copy(back[:], turned[:])
+            turn(half(src, h).bitcast(F32), back)
+            words = words_pool.tile([P, G], F32, name="words")
             for b in range(G // P):
                 s = slice(P * b, P * (b + 1))
-                nc.tensor.transpose(dst[:, s], back[:, s], identity[:])
+                nc.tensor.transpose(words[:, s], back[:, s], identity[:])
+            return words[:].bitcast(BF16)
 
-        def add_from_psum(dst, a, b):
-            for h in range(2):
-                s = slice(2 * G * h, 2 * G * (h + 1))
-                words = flips.tile([P, G], F32, name="words")
-                through_tensor(words, b[:, s].bitcast(F32))
-                nc.vector.tensor_tensor(dst[:, s], words[:].bitcast(BF16), a[:, s], ADD)
+        def vector_add(dst, a, words, h):
+            nc.vector.tensor_tensor(half(dst, h), words, half(a, h), ADD)
+
+        raws = {}
+        LOW, HIGH, ALL = slice(0, 2), slice(2, 4), slice(0, 4)
+
+        def open_step(i, o):
+            raws[i, o] = stage.tile([P, 4, T], F32, name="raw")
+            gathered[i, o] = ring.tile([P, 4 * G], BF16, name="g")
+
+        def load(i, o, rows):
+            src = cb[o, PASS * i : PASS * (i + 1), :].rearrange("(p j) c -> p j c", j=4)
+            nc.sync.dma_start(raws[i, o][:, rows, :], src[:, rows, :])
+
+        def pack(i, o, h, on_vector=False):
+            table = tables[(O * i + o) % N_TABLES]
+            dst = table[:, h, : 2 * T].rearrange("p (c e) -> p c e", e=2)
+            part = raws[i, o][:, 2 * h : 2 * h + 2, :].rearrange("p e c -> p c e")
+            if on_vector:
+                nc.vector.tensor_copy(dst, part)
+            else:
+                nc.scalar.activation(dst, part, COPY)
+
+        def gather(i, o, h):
+            table = tables[(O * i + o) % N_TABLES]
+            offsets = lists[:, (G // 16) * o : (G // 16) * (o + 1)]
+            nc.vector.tensor_copy(half(gathered[i, o], h).bitcast(U32), table[:, h, :].bitcast(U32).indirect(offsets))
 
         def load_and_gather(i, o):
-            step = O * i + o
-            raw = stage.tile([P, 4, T], F32, name="raw")
-            src = cb[o, PASS * i : PASS * (i + 1), :].rearrange("(p j) c -> p j c", j=4)
-            table = tables[step % N_TABLES]
-            if step == 0:
-                for h in range(2):
-                    nc.sync.dma_start(raw[:, 2 * h : 2 * h + 2, :], src[:, 2 * h : 2 * h + 2, :])
-                for h in range(2):
-                    dst = table[:, 2 * T * h : 2 * T * (h + 1)].rearrange("p (c e) -> p c e", e=2)
-                    part = raw[:, 2 * h : 2 * h + 2, :].rearrange("p e c -> p c e")
-                    if h == 0:
-                        nc.vector.tensor_copy(dst, part)
-                    else:
-                        nc.scalar.activation(dst, part, COPY)
-            else:
-                nc.sync.dma_start(raw[:], src)
-                for h in range(2):
-                    dst = table[:, 2 * T * h : 2 * T * (h + 1)].rearrange("p (c e) -> p c e", e=2)
-                    part = raw[:, 2 * h : 2 * h + 2, :].rearrange("p e c -> p c e")
-                    nc.scalar.activation(dst, part, COPY)
-            g = ring.tile([P, 4 * G], BF16, name="g")
-            offsets = lists[:, (G // 16) * o : (G // 16) * (o + 1)]
+            open_step(i, o)
+            for rows in (LOW, HIGH) if i == 0 and o == 2 else (ALL,):
+                load(i, o, rows)
             for h in range(2):
-                window = table[:, 2 * T * h : 2 * (T * h + WINDOW)].bitcast(U32)
-                nc.vector.tensor_copy(g[:, 2 * G * h : 2 * G * (h + 1)].bitcast(U32), window.indirect(offsets))
-            gathered[i, o] = g
+                pack(i, o, h)
+            for h in range(2):
+                gather(i, o, h)
 
-        def add_on(engine, dst, a, b):
+        def head():
+            for o in range(2):
+                open_step(0, o)
+            load(0, 0, LOW)
+            nc.sync.dma_start(lists[:], offs)
+            load(0, 1, LOW)
+            load(0, 0, HIGH)
+            load(0, 1, HIGH)
             for h in range(2):
-                s = slice(2 * G * h, 2 * G * (h + 1))
-                engine.tensor_tensor(dst[:, s], a[:, s], b[:, s], ADD)
+                for o in range(2):
+                    pack(0, o, h, on_vector=h == 0)
+                    gather(0, o, h)
 
         def gpsimd_step(i, o):
-            if o == 1:
-                add_on(nc.gpsimd, acc_g[i], gathered[i, 0], gathered[i, 1])
-            elif 1 < o <= ON_GPSIMD[i]:
-                add_on(nc.gpsimd, acc_g[i], acc_g[i], gathered[i, o])
+            for h in range(2):
+                if 1 <= o <= ON_GPSIMD[i]:
+                    first = gathered[i, 0] if o == 1 else acc_g[i]
+                    nc.gpsimd.tensor_tensor(half(acc_g[i], h), half(first, h), half(gathered[i, o], h), ADD)
+
+        def scale_turned(i):
+            planes = total[i][:].rearrange("p (h c e) -> p h c e", h=2, e=2)
+            for b in range(G // P):
+                turned = flips.tile([P, 4 * P], F32, name="turned")
+                for t in range(4):
+                    nc.tensor.transpose(turned[:, P * t : P * (t + 1)], planes[:, t // 2, P * b : P * (b + 1), t % 2], identity[:])
+                mid = middle[b % 2]
+                nc.scalar.activation(mid[:], turned[:], COPY, scale=norm_turned[:, P * b : P * b + 1])
+                back = words_pool.tile([P, 4 * P], BF16, name="back_bf", tag="words")
+                for t in range(4):
+                    nc.tensor.transpose(back[:, P * t : P * (t + 1)], mid[:, P * t : P * (t + 1)], identity_bf[:])
+                nc.scalar.copy(
+                    e_bf[i][:, 4 * P * b : 4 * P * (b + 1)].rearrange("p (c t) -> p c t", t=4),
+                    back[:].rearrange("p (t c) -> p c t", t=4),
+                )
 
         def scale_quantise(i, c0, c1):
             n = c1 - c0
             src = total[i][:].rearrange("p (h c e) -> p c h e", h=2, e=2)[:, c0:c1]
-            by = norm_ps[:, c0:c1].unsqueeze(2).unsqueeze(3).to_broadcast([P, n, 2, 2])
+            by = norm_sb[:, c0:c1].unsqueeze(2).unsqueeze(3).to_broadcast([P, n, 2, 2])
             dst = e_bf[i][:, 4 * c0 : 4 * c1].rearrange("p (c h e) -> p c h e", h=2, e=2)
             nc.vector.tensor_tensor(dst, src, by, MULT)
             nc.vector.quantize_mx(e_codes[i][:, c0:c1].bitcast(FP8X4), e_scales[i][:, c0:c1], e_bf[i][:, 4 * c0 : 4 * c1])
@@ -139,38 +175,49 @@ def tile_attend_aq_kernel(tc, cb, w, norm, offs, out):
                 stop=(i == N_PASS - 1),
             )
 
-        for o in range(O):
+        g = gathered
+        head()
+        gpsimd_step(0, 1)
+        for o in range(2, O):
             load_and_gather(0, o)
             gpsimd_step(0, o)
-            if o == 2:
-                nc.sync.dma_start(w_raw[:], w.rearrange("(i p j) m -> p i j m", i=N_PASS, j=4))
-                nc.sync.dma_start(norm_sb[:], norm)
-                through_tensor(norm_ps, norm_sb)
-            if o == 5:
-                nc.scalar.activation(
-                    w_bf[:].rearrange("p (i m j) -> p i m j", i=N_PASS, j=4),
-                    w_raw[:].rearrange("p i j m -> p i m j"),
-                    COPY,
-                )
-                nc.vector.quantize_mx(w_codes[:].bitcast(FP8X4), w_scales[:], w_bf[:])
 
         for o in range(O):
             load_and_gather(1, o)
-            gpsimd_step(1, o)
             if o == 0:
-                add_from_psum(acc_v[0], gathered[0, 6], gathered[0, 5])
-                add_from_psum(acc_v[0], acc_v[0], gathered[0, 7])
-                add_on(nc.gpsimd, acc_g[0], acc_g[0], acc_v[0])
-            if o == 5:
-                scale_quantise(0, 0, G)
-                multiply(0, 0)
-                multiply(0, 1)
+                for h in range(2):
+                    vector_add(acc_v[0], g[0, 7], to_psum(g[0, 6], h), h)
+                for h in range(2):
+                    nc.gpsimd.tensor_tensor(half(acc_g[0], h), half(acc_g[0], h), half(acc_v[0], h), ADD)
+            gpsimd_step(1, o)
+            if o == 2:
+                nc.sync.dma_start(norm_sb[:], norm)
+                nc.sync.dma_start(w_raw[:], w.rearrange("(i p j) m -> p i j m", i=N_PASS, j=4))
+            if o == 4:
+                for h in range(2):
+                    vector_add(acc_v[1], g[1, 4], to_psum(g[1, 3], h), h)
             if o == 6:
-                add_from_psum(acc_v[1], gathered[1, 6], gathered[1, 5])
-        add_on(nc.vector, acc_v[1], acc_v[1], acc_g[1])
+                for h in range(2):
+                    vector_add(acc_v[1], acc_v[1], to_psum(g[1, 5], h), h)
+                for h in range(2):
+                    nc.gpsimd.tensor_tensor(half(acc_g[1], h), half(acc_g[1], h), half(acc_v[1], h), ADD)
+        sixth = [to_psum(g[1, 6], h) for h in range(2)]
+        turn(norm_sb, norm_turned)
+        scale_turned(0)
+        nc.scalar.activation(
+            w_bf[:].rearrange("p (i m j) -> p i m j", i=N_PASS, j=4),
+            w_raw[:].rearrange("p i j m -> p i m j"),
+            COPY,
+        )
+        for h in range(2):
+            vector_add(acc_v[0], g[1, 7], sixth[h], h)
+        nc.vector.quantize_mx(w_codes[:].bitcast(FP8X4), w_scales[:], w_bf[:])
+        nc.vector.quantize_mx(e_codes[0][:].bitcast(FP8X4), e_scales[0][:], e_bf[0][:])
+        multiply(0, 0)
+        multiply(0, 1)
         halves = lambda t, b: t[:].rearrange("p (h c) -> p h c", h=2)[:, :, G * b : G * (b + 1)]
         for b in range(2):
-            nc.vector.tensor_tensor(halves(acc_v[1], b), halves(acc_v[1], b), halves(gathered[1, 7], b), ADD)
+            nc.vector.tensor_tensor(halves(acc_v[0], b), halves(acc_v[0], b), halves(acc_g[1], b), ADD)
         for b in range(2):
             scale_quantise(1, HALF * b, HALF * (b + 1))
             multiply(1, b)

@@ -21,7 +21,7 @@ COPY = mybir.ActivationFunctionType.Copy
 
 WINDOW = 688
 N_TABLES = 8
-ON_GPSIMD = (5, 2)
+ON_GPSIMD = (5, 4)
 HALF = G // 2
 
 
@@ -44,7 +44,7 @@ def tile_attend_aq_kernel(tc, cb, w, norm, offs, out):
         identity = keep.tile([P, P], F32, name="identity")
         make_identity(nc, identity[:])
         identity_bf = keep.tile([P, P], BF16, name="identity_bf")
-        make_identity(nc, identity_bf[:])
+        nc.scalar.copy(identity_bf[:], identity[:])
         norm_turned = keep.tile([P, G], F32, name="norm_turned")
         middle = [keep.tile([P, G], BF16, name=f"middle{i}") for i in range(2)]
         norm_sb = keep.tile([P, G], F32, name="norm_sb")
@@ -83,7 +83,7 @@ def tile_attend_aq_kernel(tc, cb, w, norm, offs, out):
             return words[:].bitcast(BF16)
 
         def vector_add(dst, a, words, h):
-            nc.vector.tensor_tensor(half(dst, h), words, half(a, h), ADD)
+            nc.vector.tensor_tensor(half(dst, h), half(a, h), words, ADD)
 
         raws = {}
         LOW, HIGH, ALL = slice(0, 2), slice(2, 4), slice(0, 4)
@@ -132,11 +132,13 @@ def tile_attend_aq_kernel(tc, cb, w, norm, offs, out):
                     pack(0, o, h, on_vector=h == 0)
                     gather(0, o, h)
 
-        def gpsimd_step(i, o):
+        def gpsimd_add(dst, a, b, h):
+            nc.gpsimd.tensor_tensor(half(dst, h), half(a, h), half(b, h), ADD)
+
+        def gpsimd_step(o):
             for h in range(2):
-                if 1 <= o <= ON_GPSIMD[i]:
-                    first = gathered[i, 0] if o == 1 else acc_g[i]
-                    nc.gpsimd.tensor_tensor(half(acc_g[i], h), half(first, h), half(gathered[i, o], h), ADD)
+                if o <= ON_GPSIMD[h]:
+                    gpsimd_add(acc_g[0], g[0, 0] if o == 1 else acc_g[0], g[0, o], h)
 
         def scale_turned(i):
             planes = total[i][:].rearrange("p (h c e) -> p h c e", h=2, e=2)
@@ -154,12 +156,14 @@ def tile_attend_aq_kernel(tc, cb, w, norm, offs, out):
                     back[:].rearrange("p (t c) -> p c t", t=4),
                 )
 
-        def scale_quantise(i, c0, c1):
+        def scale(i, c0, c1):
             n = c1 - c0
             src = total[i][:].rearrange("p (h c e) -> p c h e", h=2, e=2)[:, c0:c1]
             by = norm_sb[:, c0:c1].unsqueeze(2).unsqueeze(3).to_broadcast([P, n, 2, 2])
             dst = e_bf[i][:, 4 * c0 : 4 * c1].rearrange("p (c h e) -> p c h e", h=2, e=2)
             nc.vector.tensor_tensor(dst, src, by, MULT)
+
+        def quantise(i, c0, c1):
             nc.vector.quantize_mx(e_codes[i][:, c0:c1].bitcast(FP8X4), e_scales[i][:, c0:c1], e_bf[i][:, 4 * c0 : 4 * c1])
 
         def multiply(i, b):
@@ -177,33 +181,32 @@ def tile_attend_aq_kernel(tc, cb, w, norm, offs, out):
 
         g = gathered
         head()
-        gpsimd_step(0, 1)
+        gpsimd_step(1)
         for o in range(2, O):
             load_and_gather(0, o)
-            gpsimd_step(0, o)
+            gpsimd_step(o)
 
         for o in range(O):
             load_and_gather(1, o)
             if o == 0:
                 for h in range(2):
                     vector_add(acc_v[0], g[0, 7], to_psum(g[0, 6], h), h)
+                vector_add(acc_v[0], acc_v[0], to_psum(g[0, 5], 1), 1)
                 for h in range(2):
-                    nc.gpsimd.tensor_tensor(half(acc_g[0], h), half(acc_g[0], h), half(acc_v[0], h), ADD)
-            gpsimd_step(1, o)
+                    gpsimd_add(acc_g[0], acc_g[0], acc_v[0], h)
             if o == 2:
                 nc.sync.dma_start(norm_sb[:], norm)
                 nc.sync.dma_start(w_raw[:], w.rearrange("(i p j) m -> p i j m", i=N_PASS, j=4))
-            if o == 4:
                 for h in range(2):
-                    vector_add(acc_v[1], g[1, 4], to_psum(g[1, 3], h), h)
-            if o == 6:
+                    vector_add(acc_v[1], g[1, 1], to_psum(g[1, 0], h), h)
                 for h in range(2):
-                    vector_add(acc_v[1], acc_v[1], to_psum(g[1, 5], h), h)
+                    vector_add(acc_v[1], acc_v[1], to_psum(g[1, 2], h), h)
+            if o in (3, 4, 5):
                 for h in range(2):
-                    nc.gpsimd.tensor_tensor(half(acc_g[1], h), half(acc_g[1], h), half(acc_v[1], h), ADD)
-        sixth = [to_psum(g[1, 6], h) for h in range(2)]
+                    gpsimd_add(acc_g[1], acc_v[1] if o == 3 else acc_g[1], g[1, o], h)
         turn(norm_sb, norm_turned)
         scale_turned(0)
+        sixth = [to_psum(g[1, 6], h) for h in range(2)]
         nc.scalar.activation(
             w_bf[:].rearrange("p (i m j) -> p i m j", i=N_PASS, j=4),
             w_raw[:].rearrange("p i j m -> p i m j"),
@@ -211,15 +214,18 @@ def tile_attend_aq_kernel(tc, cb, w, norm, offs, out):
         )
         for h in range(2):
             vector_add(acc_v[0], g[1, 7], sixth[h], h)
-        nc.vector.quantize_mx(w_codes[:].bitcast(FP8X4), w_scales[:], w_bf[:])
-        nc.vector.quantize_mx(e_codes[0][:].bitcast(FP8X4), e_scales[0][:], e_bf[0][:])
-        multiply(0, 0)
-        multiply(0, 1)
         halves = lambda t, b: t[:].rearrange("p (h c) -> p h c", h=2)[:, :, G * b : G * (b + 1)]
         for b in range(2):
             nc.vector.tensor_tensor(halves(acc_v[0], b), halves(acc_v[0], b), halves(acc_g[1], b), ADD)
+        quantise(0, 0, G)
+        scale(1, 0, HALF)
+        nc.vector.quantize_mx(w_codes[:].bitcast(FP8X4), w_scales[:], w_bf[:])
+        multiply(0, 0)
+        multiply(0, 1)
         for b in range(2):
-            scale_quantise(1, HALF * b, HALF * (b + 1))
+            if b:
+                scale(1, HALF, G)
+            quantise(1, HALF * b, HALF * (b + 1))
             multiply(1, b)
             nc.scalar.activation(out_sb[b][:], banks[b][:], COPY)
             nc.sync.dma_start(out[:, HALF * b : HALF * (b + 1)], out_sb[b][:])

from contextlib import ExitStack

import concourse.mybir as mybir
from concourse.masks import make_identity

O, G, T, D, M = 8, 512, 512, 1024, 128
P = 128
PASS = 512
N_PASS = D // PASS
FLOPS = 2 * D * M * G

F32 = mybir.dt.float32
BF16 = mybir.dt.bfloat16
U32 = mybir.dt.uint32
U16 = mybir.dt.uint16
U8 = mybir.dt.uint8
FP8X4 = mybir.dt.float8_e4m3fn_x4
ADD = mybir.AluOpType.add
MULT = mybir.AluOpType.mult
COPY = mybir.ActivationFunctionType.Copy

WINDOW = 688
N_TABLES = 8
ON_GPSIMD = (5, 4)
HALF = G // 2


def tile_attend_aq_kernel(tc, cb, w, norm, offs, out):
    nc = tc.nc
    with ExitStack() as ctx:
        keep = ctx.enter_context(tc.tile_pool(name="keep", bufs=1))
        stage = ctx.enter_context(tc.tile_pool(name="stage", bufs=6))
        ring = ctx.enter_context(tc.tile_pool(name="ring", bufs=16))
        psum = ctx.enter_context(tc.psum_pool(name="psum", bufs=1))
        words_pool = ctx.enter_context(tc.psum_pool(name="words_pool", bufs=4))
        flips = ctx.enter_context(tc.psum_pool(name="flips", bufs=2))

        lists = keep.tile([P, O * G // 16], U16, name="lists")

        tables = [keep.tile([P, 2, 2 * WINDOW], BF16, name=f"table{i}") for i in range(N_TABLES)]
        for t in tables:
            nc.gpsimd.memset(t[:, :, 2 * T :].bitcast(U32), 0)

        identity = keep.tile([P, P], F32, name="identity")
        make_identity(nc, identity[:])
        identity_bf = keep.tile([P, P], BF16, name="identity_bf")
        nc.scalar.copy(identity_bf[:], identity[:])
        norm_turned = keep.tile([P, G], F32, name="norm_turned")
        middle = [keep.tile([P, G], BF16, name=f"middle{i}") for i in range(2)]
        norm_sb = keep.tile([P, G], F32, name="norm_sb")
        w_raw = keep.tile([P, N_PASS, 4, M], F32, name="w_raw")
        w_bf = keep.tile([P, N_PASS * M * 4], BF16, name="w_bf", align_bytes=64)
        w_codes = keep.tile([P, N_PASS * M], U32, name="w_codes", align_bytes=64)
        w_scales = keep.tile([P, N_PASS * M], U8, name="w_scales", align_bytes=64)

        acc_g = [keep.tile([P, 4 * G], F32, name=f"acc_g{i}") for i in range(N_PASS)]
        acc_v = [keep.tile([P, 4 * G], F32, name=f"acc_v{i}") for i in range(N_PASS)]
        e_bf = [keep.tile([P, 4 * G], BF16, name=f"e_bf{i}", align_bytes=64) for i in range(N_PASS)]
        e_codes = [keep.tile([P, G], U32, name=f"e_codes{i}", align_bytes=64) for i in range(N_PASS)]
        e_scales = [keep.tile([P, G], U8, name=f"e_scales{i}", align_bytes=64) for i in range(N_PASS)]
        banks = [psum.tile([M, HALF], F32, name=f"bank{i}") for i in range(2)]
        out_sb = [keep.tile([M, HALF], F32, name=f"out_sb{i}") for i in range(2)]
        total = (acc_g[0], acc_v[0])
        gathered = {}

        def turn(src, dst):
            turned = flips.tile([P, G], F32, name="turned")
            for b in range(G // P):
                s = slice(P * b, P * (b + 1))
                nc.tensor.transpose(turned[:, s], src[:, s], identity[:])
            nc.scalar.copy(dst[:], turned[:])

        def half(t, h):
            return t[:, 2 * G * h : 2 * G * (h + 1)]

        def to_psum(src, h):
            back = stage.tile([P, G], F32, name="back")
            turn(half(src, h).bitcast(F32), back)
            words = words_pool.tile([P, G], F32, name="words")
            for b in range(G // P):
                s = slice(P * b, P * (b + 1))
                nc.tensor.transpose(words[:, s], back[:, s], identity[:])
            return words[:].bitcast(BF16)

        def vector_add(dst, a, words, h):
            nc.vector.tensor_tensor(half(dst, h), half(a, h), words, ADD)

        raws = {}
        LOW, HIGH, ALL = slice(0, 2), slice(2, 4), slice(0, 4)

        def open_step(i, o):
            raws[i, o] = stage.tile([P, 4, T], F32, name="raw")
            gathered[i, o] = ring.tile([P, 4 * G], BF16, name="g")

        def load(i, o, rows):
            src = cb[o, PASS * i : PASS * (i + 1), :].rearrange("(p j) c -> p j c", j=4)
            nc.sync.dma_start(raws[i, o][:, rows, :], src[:, rows, :])

        def pack(i, o, h, on_vector=False):
            table = tables[(O * i + o) % N_TABLES]
            dst = table[:, h, : 2 * T].rearrange("p (c e) -> p c e", e=2)
            part = raws[i, o][:, 2 * h : 2 * h + 2, :].rearrange("p e c -> p c e")
            if on_vector:
                nc.vector.tensor_copy(dst, part)
            else:
                nc.scalar.activation(dst, part, COPY)

        def gather(i, o, h):
            table = tables[(O * i + o) % N_TABLES]
            offsets = lists[:, (G // 16) * o : (G // 16) * (o + 1)]
            nc.vector.tensor_copy(half(gathered[i, o], h).bitcast(U32), table[:, h, :].bitcast(U32).indirect(offsets))

        def load_and_gather(i, o):
            open_step(i, o)
            for rows in (LOW, HIGH) if i == 0 and o == 2 else (ALL,):
                load(i, o, rows)
            for h in range(2):
                pack(i, o, h)
            for h in range(2):
                gather(i, o, h)

        def head():
            for o in range(2):
                open_step(0, o)
            load(0, 0, LOW)
            nc.sync.dma_start(lists[:], offs)
            load(0, 1, LOW)
            load(0, 0, HIGH)
            load(0, 1, HIGH)
            for h in range(2):
                for o in range(2):
                    pack(0, o, h, on_vector=h == 0)
                    gather(0, o, h)

        def gpsimd_add(dst, a, b, h):
            nc.gpsimd.tensor_tensor(half(dst, h), half(a, h), half(b, h), ADD)

        def gpsimd_step(o):
            for h in range(2):
                if o <= ON_GPSIMD[h]:
                    gpsimd_add(acc_g[0], g[0, 0] if o == 1 else acc_g[0], g[0, o], h)

        def scale_turned(i):
            planes = total[i][:].rearrange("p (h c e) -> p h c e", h=2, e=2)
            for b in range(G // P):
                turned = flips.tile([P, 4 * P], F32, name="turned")
                for t in range(4):
                    nc.tensor.transpose(turned[:, P * t : P * (t + 1)], planes[:, t // 2, P * b : P * (b + 1), t % 2], identity[:])
                mid = middle[b % 2]
                nc.scalar.activation(mid[:], turned[:], COPY, scale=norm_turned[:, P * b : P * b + 1])
                back = words_pool.tile([P, 4 * P], BF16, name="back_bf", tag="words")
                for t in range(4):
                    nc.tensor.transpose(back[:, P * t : P * (t + 1)], mid[:, P * t : P * (t + 1)], identity_bf[:])
                nc.scalar.copy(
                    e_bf[i][:, 4 * P * b : 4 * P * (b + 1)].rearrange("p (c t) -> p c t", t=4),
                    back[:].rearrange("p (t c) -> p c t", t=4),
                )

        def scale(i, c0, c1):
            n = c1 - c0
            src = total[i][:].rearrange("p (h c e) -> p c h e", h=2, e=2)[:, c0:c1]
            by = norm_sb[:, c0:c1].unsqueeze(2).unsqueeze(3).to_broadcast([P, n, 2, 2])
            dst = e_bf[i][:, 4 * c0 : 4 * c1].rearrange("p (c h e) -> p c h e", h=2, e=2)
            nc.vector.tensor_tensor(dst, src, by, MULT)

        def quantise(i, c0, c1):
            nc.vector.quantize_mx(e_codes[i][:, c0:c1].bitcast(FP8X4), e_scales[i][:, c0:c1], e_bf[i][:, 4 * c0 : 4 * c1])

        def multiply(i, b):
            c = slice(HALF * b, HALF * (b + 1))
            m = slice(M * i, M * (i + 1))
            nc.tensor.matmul_mx(
                out=banks[b][:],
                lhsT=w_codes[:, m].bitcast(FP8X4),
                lhsT_scale=w_scales[:, m],
                rhs=e_codes[i][:, c].bitcast(FP8X4),
                rhs_scale=e_scales[i][:, c],
                start=(i == 0),
                stop=(i == N_PASS - 1),
            )

        g = gathered
        head()
        gpsimd_step(1)
        for o in range(2, O):
            load_and_gather(0, o)
            gpsimd_step(o)

        for o in range(O):
            load_and_gather(1, o)
            if o == 0:
                for h in range(2):
                    vector_add(acc_v[0], g[0, 7], to_psum(g[0, 6], h), h)
                vector_add(acc_v[0], acc_v[0], to_psum(g[0, 5], 1), 1)
                for h in range(2):
                    gpsimd_add(acc_g[0], acc_g[0], acc_v[0], h)
            if o == 2:
                nc.sync.dma_start(norm_sb[:], norm)
                nc.sync.dma_start(w_raw[:], w.rearrange("(i p j) m -> p i j m", i=N_PASS, j=4))
                for h in range(2):
                    vector_add(acc_v[1], g[1, 1], to_psum(g[1, 0], h), h)
                for h in range(2):
                    vector_add(acc_v[1], acc_v[1], to_psum(g[1, 2], h), h)
            if o in (3, 4, 5):
                for h in range(2):
                    gpsimd_add(acc_g[1], acc_v[1] if o == 3 else acc_g[1], g[1, o], h)
        turn(norm_sb, norm_turned)
        scale_turned(0)
        sixth = [to_psum(g[1, 6], h) for h in range(2)]
        nc.scalar.activation(
            w_bf[:].rearrange("p (i m j) -> p i m j", i=N_PASS, j=4),
            w_raw[:].rearrange("p i j m -> p i m j"),
            COPY,
        )
        for h in range(2):
            vector_add(acc_v[0], g[1, 7], sixth[h], h)
        halves = lambda t, b: t[:].rearrange("p (h c) -> p h c", h=2)[:, :, G * b : G * (b + 1)]
        for b in range(2):
            nc.vector.tensor_tensor(halves(acc_v[0], b), halves(acc_v[0], b), halves(acc_g[1], b), ADD)
        quantise(0, 0, G)
        scale(1, 0, HALF)
        nc.vector.quantize_mx(w_codes[:].bitcast(FP8X4), w_scales[:], w_bf[:])
        multiply(0, 0)
        multiply(0, 1)
        for b in range(2):
            if b:
                scale(1, HALF, G)
            quantise(1, HALF * b, HALF * (b + 1))
            multiply(1, b)
            nc.scalar.activation(out_sb[b][:], banks[b][:], COPY)
            nc.sync.dma_start(out[:, HALF * b : HALF * (b + 1)], out_sb[b][:])
